import numpy as np
import ml_dtypes


def mxq(x, axis, fmt="e4m3"):
    dtype, down = {"e4m3": (ml_dtypes.float8_e4m3fn, 7), "e5m2": (ml_dtypes.float8_e5m2, 14)}[fmt]
    v = np.moveaxis(np.asarray(x, np.float32).astype(ml_dtypes.bfloat16).astype(np.float64), axis, -1)
    blocks = v.reshape(v.shape[:-1] + (-1, 32))
    amax = np.abs(blocks).max(-1, keepdims=True)
    byte = np.maximum(np.where(amax > 0, np.frexp(amax)[1] - 1 + 127, 0) - down, 1)
    scale = np.exp2(byte - 127.0)
    codes = (blocks / scale).astype(np.float32).astype(dtype).astype(np.float64)
    return np.moveaxis((codes * scale).reshape(v.shape), -1, axis)


WIDE = False


def mx_kscale(k):
    if not WIDE:
        return np.ones(k)
    levels = np.array([10, -10, 5, -5, 0])
    if k % 512:
        return np.exp2(np.random.permutation(np.resize(levels, k // 32))).repeat(32)
    a = np.empty((k // 512, 16))
    for p in range(k // 512):
        a[p, :8] = np.random.permutation(np.resize(levels, 8))
        for g in range(8):
            far = levels[np.abs(levels - a[p, g]) >= 10]
            a[p, g + 8] = far[np.random.randint(len(far))]
    return np.exp2(a.ravel()).repeat(32)


def f64(x):
    return np.asarray(x).astype(np.float64)


def striped(idx):
    return np.tile(np.asarray(idx).reshape(-1, 16).T, (8, 1)).astype(np.uint16)


def unstriped(offs):
    return offs[:16].T.reshape(-1).astype(np.int64)


E2M1 = np.array([0.0, 0.5, 1.0, 1.5, 2.0, 3.0, 4.0, 6.0, -0.0, -0.5, -1.0, -1.5, -2.0, -3.0, -4.0, -6.0])


def pack_weight(w, fmt):
    k, n = w.shape
    w = f64(np.asarray(w, np.float32).astype(ml_dtypes.bfloat16)).reshape(k // 32, 32, n)
    amax = np.abs(w).max(1)
    if fmt == "e4m3":
        byte = np.frexp(amax)[1] - 1 + 127 - 7
    else:
        mant, ex = np.frexp(amax / 6.0)
        byte = np.where(mant > 0.5, ex, ex - 1) + 127
    byte = np.clip(np.where(amax > 0, byte, 1), 1, 254)
    scaled = (w * np.exp2(127.0 - byte)[:, None, :]).reshape(k, n).astype(np.float32)
    by_word = np.ascontiguousarray(scaled.reshape(k // 512, 128, 4, n).transpose(0, 1, 3, 2))
    if fmt == "e4m3":
        words = by_word.astype(ml_dtypes.float8_e4m3fn).view(np.uint8)
    else:
        c = by_word.astype(ml_dtypes.float4_e2m1fn).view(np.uint8) & 0xF
        words = (c[..., 0::2] | (c[..., 1::2] << 4)).reshape(k // 512, 128, 2 * n)
    return np.ascontiguousarray(words), np.ascontiguousarray(byte.astype(np.uint8).reshape(k // 512, 16, n))


def unpack_weight(words, scales, fmt):
    g, _, n = scales.shape
    words = np.ascontiguousarray(words).reshape(g, 128, n, -1)
    if fmt == "e4m3":
        vals = words.view(ml_dtypes.float8_e4m3fn).astype(np.float64)
    else:
        nib = np.empty((g, 128, n, 4), np.uint8)
        nib[..., 0::2] = words & 0xF
        nib[..., 1::2] = words >> 4
        vals = E2M1[nib]
    vals = vals * np.repeat(np.exp2(scales.astype(np.float64) - 127.0), 8, axis=1)[..., None]
    return vals.transpose(0, 1, 3, 2).reshape(g * 512, n)


B, N, T, D, DV, NQ = 1, 512, 1024, 1024, 256, 256


def setup_inputs():
    n = np.random.standard_normal
    idx = np.sort(np.random.permutation(T)[:B * N].reshape(B, N), axis=1).reshape(-1)
    s = mx_kscale(D)[:, None]
    u = np.ones(T)
    u[idx] = mx_kscale(B * N)
    r = np.random.uniform(0.5, 2.0, T)
    qp = [pack_weight(x, "e4m3") for x in n((B, D, NQ)) * s * (0.80 / np.sqrt(D))]
    k = n((D, T)) / s
    v = n((DV, T)) / (u * r)
    kp = pack_weight(k, "e4m3")
    when = np.zeros(T)
    when[idx] = np.sort(np.random.permutation(2 * N)[:B * N])
    return {
        "q_words": np.stack([x[0] for x in qp]),
        "q_scales": np.stack([x[1] for x in qp]),
        "k_words": kp[0],
        "k_scales": kp[1],
        "vT": v.astype(np.float32),
        "vs": np.tile(u * r, (128, 1)).astype(np.float32),
        "pos": np.tile(when, (128, 1)).astype(np.float32),
        "slope": np.exp2(-np.random.randint(8, 13, (B, NQ, 1))).astype(np.float32),
        "sink": (2.0 + 3.0 * n((B, NQ, 1))).astype(np.float32),
        "offs": striped(idx),
    }


def reference(q_words, q_scales, k_words, k_scales, vT, vs, pos, slope, sink, offs):
    idx = unstriped(offs)
    k = unpack_weight(k_words, k_scales, "e4m3")
    v = f64(vT)
    pick = lambda x: x[:, idx].reshape(x.shape[0], B, N).transpose(1, 0, 2)
    q = np.stack([unpack_weight(q_words[b], q_scales[b], "e4m3") for b in range(B)])
    score = q.transpose(0, 2, 1) @ pick(k)
    score = score + f64(slope) * pick(f64(pos))[:, :1, :]
    m = np.maximum(score.max(-1, keepdims=True), f64(sink))
    p = np.exp(score - m)
    total = p.sum(-1, keepdims=True) + np.exp(f64(sink) - m)
    w = p * pick(f64(vs))[:, :1, :]
    y = mxq(w, 2, "e4m3") @ mxq(pick(v).transpose(0, 2, 1), 1, "e4m3")
    y = y / total
    return y

@@ -1,0 +1,174 @@
+from contextlib import ExitStack
+
+import concourse.mybir as mybir
+from concourse.masks import make_identity
+
+F32 = mybir.dt.float32
+BF16 = mybir.dt.bfloat16
+I32 = mybir.dt.int32
+U32 = mybir.dt.uint32
+U16 = mybir.dt.uint16
+U8 = mybir.dt.uint8
+FP8X4 = mybir.dt.float8_e4m3fn_x4
+ALU = mybir.AluOpType
+ACT = mybir.ActivationFunctionType
+AXIS = mybir.AxisListType
+
+P = 128
+PACK = 4
+N, T, D, DV, NQ = 512, 1024, 1024, 256, 256
+PASSES = D // (P * PACK)
+BLOCKS = NQ // P
+FLOPS = 2 * NQ * N * (D + DV)
+
+
+def tile_attend_soft_alibi_sink_srtq256n512t1024_kernel(tc, q_words, q_scales, k_words, k_scales, vT, vs, pos, slope, sink, offs, out):
+    nc = tc.nc
+    with ExitStack() as ctx:
+        sb = ctx.enter_context(tc.tile_pool(name="sb", bufs=1))
+        ps = ctx.enter_context(tc.psum_pool(name="ps", bufs=1))
+
+        offsets = sb.tile([P, N // 16], U16, name="offsets")
+        nc.sync.dma_start(offsets[:], offs)
+
+        ks_pool = sb.tile([P, T], U8, name="ks_pool", align_bytes=64)
+        qs = sb.tile([P, NQ], U8, name="qs", align_bytes=64)
+        rows = sb.tile([P, P], F32, name="rows")
+        nc.gpsimd.memset(ks_pool[:].bitcast(I32), 0)
+        nc.vector.memset(qs[:].bitcast(I32), 0)
+        nc.vector.memset(rows[:], 0.0)
+        full = sb.tile([P, BLOCKS], F32, name="full")
+        warm = sb.tile([P, 1], F32, name="warm")
+        nc.vector.memset(warm[:], 0.0)
+        nc.scalar.activation(full[:, 0:1], warm[:], ACT.Exp)
+
+        kw_pool = [sb.tile([P, T], U32, name=f"kw_pool{o}") for o in range(PASSES)]
+        pos_pool = sb.tile([P, T], F32, name="pos_pool")
+        vs_pool = sb.tile([P, T], F32, name="vs_pool")
+        qw = sb.tile([P, PASSES, NQ], U32, name="qw", align_bytes=64)
+        v_raw = [sb.tile([P, 2, T // 2], F32, name=f"v_raw{c}", tag=f"v_raw{c}") for c in range(2)]
+
+        ident = sb.tile([P, P], F32, name="ident")
+        make_identity(nc, ident[:])
+        nc.gpsimd.dma_start(rows[0:BLOCKS, :], slope[0, :, 0].rearrange("(b p) -> b p", p=P))
+        nc.gpsimd.dma_start(rows[BLOCKS:2 * BLOCKS, :], sink[0, :, 0].rearrange("(b p) -> b p", p=P))
+        nc.vector.memset(vs_pool[:], 0.0)
+
+        def load_keys(o):
+            nc.sync.dma_start(kw_pool[o][:].bitcast(I32), k_words[o].rearrange("p t r -> p (t r)").bitcast(I32))
+
+        for quad in range(4):
+            nc.sync.dma_start(ks_pool[32 * quad:32 * quad + 8, :].bitcast(I32), k_scales[:, 4 * quad:4 * quad + 4, :].bitcast(I32))
+        load_keys(0)
+        load_keys(1)
+        nc.sync.dma_start(qw[:].bitcast(I32), q_words[0].rearrange("o p q r -> p o (q r)").bitcast(I32))
+        for quad in range(4):
+            nc.sync.dma_start(qs[32 * quad:32 * quad + 8, :].bitcast(I32), q_scales[0, :, 4 * quad:4 * quad + 4, :].bitcast(I32))
+        nc.sync.dma_start(vs_pool[0:1, :], vs[0:1, :])
+        nc.sync.dma_start(pos_pool[:], pos)
+        v_view = vT.rearrange("(p h) t -> p h t", h=2)
+        for c in range(2):
+            nc.sync.dma_start(v_raw[c][:], v_view[:, :, c * (T // 2):(c + 1) * (T // 2)])
+
+        rows_ps = ps.tile([P, DV], F32, name="rows_ps", tag="y_ps1")
+        nc.tensor.transpose(rows_ps[:, 0:P], rows[:], ident[:])
+        cols = sb.tile([P, 2 * BLOCKS], F32, name="cols")
+        neg_sink = sb.tile([P, BLOCKS], F32, name="neg_sink")
+        nc.scalar.copy(cols[:], rows_ps[:, 0:2 * BLOCKS])
+        nc.scalar.activation(neg_sink[:], rows_ps[:, BLOCKS:2 * BLOCKS], ACT.Copy, scale=-1.0)
+
+        kw = [sb.tile([P, N], U32, name=f"kw{o}", align_bytes=64) for o in range(PASSES)]
+        ks = sb.tile([P, N], U8, name="ks", align_bytes=64)
+        pos_g = sb.tile([P, N], F32, name="pos_g")
+        vs_g = sb.tile([P, N], F32, name="vs_g")
+        scores = [ps.tile([P, N], F32, name=f"scores{b}") for b in range(BLOCKS)]
+
+        def score_pass(o):
+            for b in range(BLOCKS):
+                rng = slice(b * P, (b + 1) * P)
+                nc.tensor.matmul_mx(out=scores[b][:], lhsT=qw[:, o, rng].bitcast(FP8X4), lhsT_scale=qs[4 * o:P, rng],
+                                    rhs=kw[o][:].bitcast(FP8X4), rhs_scale=ks[4 * o:P, :],
+                                    start=(o == 0), stop=(o == PASSES - 1))
+
+        nc.vector.tensor_copy(ks[:], ks_pool[:].indirect(offsets[:]))
+        nc.vector.tensor_copy(kw[0][:], kw_pool[0][:].indirect(offsets[:]))
+        nc.vector.tensor_copy(kw[1][:], kw_pool[1][:].indirect(offsets[:]))
+        score_pass(0)
+        score_pass(1)
+        nc.vector.tensor_copy(vs_g[:], vs_pool[:].indirect(offsets[:]))
+        nc.vector.tensor_copy(pos_g[:], pos_pool[:].indirect(offsets[:]))
+        vs_ps = ps.tile([P, PACK, P], F32, name="vs_ps")
+        for t in range(PACK):
+            nc.tensor.transpose(vs_ps[:, t, :], vs_g[:, t:N:PACK], ident[:])
+
+        v_pairs = sb.tile([P, 2 * T], BF16, name="v_pairs")
+        for c in range(2):
+            nc.scalar.activation(v_pairs[:, c * T:(c + 1) * T].rearrange("p (t h) -> p t h", h=2),
+                                 v_raw[c][:].rearrange("p h t -> p t h"), ACT.Copy)
+
+        ROW = N + 8
+        neg_m = [sb.tile([P, 1], F32, name=f"neg_m{b}") for b in range(BLOCKS)]
+        total = [sb.tile([P, 1], F32, name=f"total{b}") for b in range(BLOCKS)]
+        inv = sb.tile([P, BLOCKS], F32, name="inv")
+        p_ps = [ps.tile([P, PACK, P], F32, name=f"p_ps{b}") for b in range(BLOCKS)]
+        s = [sb.tile([P, N], F32, name=f"s{b}") for b in range(BLOCKS)]
+        neg_s = [sb.tile([P, N], F32, name=f"neg_s{b}", tag=f"neg_s{b}") for b in range(BLOCKS)]
+        p = sb.tile([P, BLOCKS * ROW], F32, name="p", tag="v_raw1")
+        for b in range(BLOCKS):
+            nc.vector.scalar_tensor_tensor(out=s[b][:], in0=pos_g[:], scalar=cols[:, b:b + 1], in1=scores[b][:],
+                                           op0=ALU.mult, op1=ALU.add)
+        for b in range(BLOCKS):
+            nc.vector.tensor_scalar(neg_s[b][:], s[b][:], -1.0, neg_sink[:, b:b + 1], ALU.mult, ALU.min, accum_out=neg_m[b][:])
+        for b in range(BLOCKS):
+            nc.scalar.activation(p[:, b * ROW:b * ROW + N].rearrange("p (t s) -> p s t", t=PACK),
+                                 neg_s[b][:].rearrange("p (s t) -> p s t", t=PACK), ACT.Exp,
+                                 bias=neg_m[b][:], scale=-1.0, accum_out=total[b][:])
+            for t in range(PACK):
+                nc.tensor.transpose(p_ps[b][:, t, :], p[:, b * ROW + t * P:b * ROW + (t + 1) * P], ident[:])
+        vs_col = sb.tile([P, PACK], F32, name="vs_col", tag="neg_s0")
+        nc.scalar.copy(vs_col[:], vs_ps[:, :, 0])
+
+        v_g = sb.tile([P, N], U32, name="v_g")
+        nc.vector.tensor_copy(v_g[:], v_pairs[:].bitcast(U32).indirect(offsets[:]))
+        v_ps = ps.tile([P, PACK, P], F32, name="v_ps")
+        for t in range(PACK):
+            nc.tensor.transpose(v_ps[:, t, :], v_g[:].bitcast(F32)[:, t:N:PACK], ident[:])
+
+        for b in range(BLOCKS):
+            sink_term = p[:, b * ROW + N:b * ROW + N + 1]
+            nc.scalar.activation(sink_term, cols[:, BLOCKS + b:BLOCKS + b + 1], ACT.Exp, bias=neg_m[b][:])
+            nc.scalar.activation(full[:, b:b + 1], total[b][:], ACT.Identity, bias=sink_term)
+
+        v_codes = sb.tile([P, DV], U32, name="v_codes", align_bytes=64)
+        v_scale = sb.tile([P, DV], U8, name="v_scale", align_bytes=64)
+        v_x = [sb.tile([P, P, PACK], BF16, name=f"v_x{h}", align_bytes=64) for h in range(2)]
+        for h in range(2):
+            nc.scalar.copy(v_x[h][:], v_ps[:].bitcast(BF16)[:, :, h * P:(h + 1) * P].rearrange("p t e -> p e t"))
+
+        w_x = [sb.tile([P, P, PACK], BF16, name=f"w_x{b}", align_bytes=64) for b in range(BLOCKS)]
+        w_codes = [sb.tile([P, P], U32, name=f"w_codes{b}", align_bytes=64) for b in range(BLOCKS)]
+        w_scale = [sb.tile([P, P], U8, name=f"w_scale{b}", align_bytes=64) for b in range(BLOCKS)]
+
+        for b in range(BLOCKS):
+            nc.vector.tensor_tensor(w_x[b][:], p_ps[b][:].rearrange("p t q -> p q t"),
+                                    vs_col[:].unsqueeze(1).broadcast_to([P, P, PACK]), ALU.mult)
+        for b in range(BLOCKS):
+            nc.vector.quantize_mx(out=w_codes[b][:].bitcast(FP8X4), scales=w_scale[b][:],
+                                  in_=w_x[b][:].rearrange("p q t -> p (q t)"))
+        nc.vector.reciprocal(inv[:], full[:])
+        for h in range(2):
+            rng = slice(h * P, (h + 1) * P)
+            nc.vector.quantize_mx(out=v_codes[:, rng].bitcast(FP8X4), scales=v_scale[:, rng],
+                                  in_=v_x[h][:].rearrange("p e t -> p (e t)"))
+
+        for b in range(BLOCKS):
+            y_ps = ps.tile([P, DV], F32, name=f"y_ps{b}", tag=f"y_ps{b}")
+            nc.tensor.matmul_mx(out=y_ps[:], lhsT=w_codes[b][:].bitcast(FP8X4), lhsT_scale=w_scale[b][:],
+                                rhs=v_codes[:].bitcast(FP8X4), rhs_scale=v_scale[:], start=True, stop=True)
+            y = sb.tile([P, DV], F32, name=f"y{b}")
+            if b == 0:
+                nc.scalar.activation(y[:], y_ps[:], ACT.Copy, scale=inv[:, b:b + 1])
+                nc.scalar.dma_start(out[0, b * P:(b + 1) * P, :], y[:])
+            else:
+                nc.vector.tensor_scalar(y[:], y_ps[:], inv[:, b:b + 1], None, ALU.mult)
+                nc.sync.dma_start(out[0, b * P:(b + 1) * P, :], y[:])

@@ -35,42 +35,41 @@ def tile_attend_soft_alibi_sink_srtq256n512t1024_kernel(tc, q_words, q_scales, k
         qs = sb.tile([P, NQ], U8, name="qs", align_bytes=64)
         rows = sb.tile([P, P], F32, name="rows")
         nc.gpsimd.memset(ks_pool[:].bitcast(I32), 0)
-        nc.vector.memset(qs[:].bitcast(I32), 0)
         nc.vector.memset(rows[:], 0.0)
-        full = sb.tile([P, BLOCKS], F32, name="full")
-        warm = sb.tile([P, 1], F32, name="warm")
-        nc.vector.memset(warm[:], 0.0)
-        nc.scalar.activation(full[:, 0:1], warm[:], ACT.Exp)
+        nc.vector.memset(qs[:].bitcast(I32), 0)
+        ident = sb.tile([P, P], F32, name="ident")
+        make_identity(nc, ident[:])
+        vs_pool = sb.tile([P, T], F32, name="vs_pool")
+        nc.gpsimd.memset(vs_pool[:], 0.0)
 
         kw_pool = [sb.tile([P, T], U32, name=f"kw_pool{o}") for o in range(PASSES)]
         pos_pool = sb.tile([P, T], F32, name="pos_pool")
-        vs_pool = sb.tile([P, T], F32, name="vs_pool")
         qw = sb.tile([P, PASSES, NQ], U32, name="qw", align_bytes=64)
-        v_raw = [sb.tile([P, 2, T // 2], F32, name=f"v_raw{c}", tag=f"v_raw{c}") for c in range(2)]
+        v_raw = [sb.tile([P, T], F32, name=f"v_raw{c}") for c in range(2)]
+        full = sb.tile([P, BLOCKS], F32, name="full")
 
-        ident = sb.tile([P, P], F32, name="ident")
-        make_identity(nc, ident[:])
-        nc.gpsimd.dma_start(rows[0:BLOCKS, :], slope[0, :, 0].rearrange("(b p) -> b p", p=P))
-        nc.gpsimd.dma_start(rows[BLOCKS:2 * BLOCKS, :], sink[0, :, 0].rearrange("(b p) -> b p", p=P))
-        nc.vector.memset(vs_pool[:], 0.0)
+        def load_scales(queue, tile, source, quad):
+            queue.dma_start(tile[32 * quad:32 * quad + 8, :].bitcast(I32), source[:, 4 * quad:4 * quad + 4, :].bitcast(I32))
 
         def load_keys(o):
             nc.sync.dma_start(kw_pool[o][:].bitcast(I32), k_words[o].rearrange("p t r -> p (t r)").bitcast(I32))
 
         for quad in range(4):
-            nc.sync.dma_start(ks_pool[32 * quad:32 * quad + 8, :].bitcast(I32), k_scales[:, 4 * quad:4 * quad + 4, :].bitcast(I32))
+            load_scales((nc.scalar, nc.sync)[quad % 2], ks_pool, k_scales, quad)
+        nc.scalar.activation(full[:, 0:1], ident[:, 0:1], ACT.Exp)
         load_keys(0)
+        nc.sync.dma_start(rows[0:BLOCKS, :], slope[0, :, 0].rearrange("(b p) -> b p", p=P))
+        nc.sync.dma_start(rows[BLOCKS:2 * BLOCKS, :], sink[0, :, 0].rearrange("(b p) -> b p", p=P))
         load_keys(1)
         nc.sync.dma_start(qw[:].bitcast(I32), q_words[0].rearrange("o p q r -> p o (q r)").bitcast(I32))
         for quad in range(4):
-            nc.sync.dma_start(qs[32 * quad:32 * quad + 8, :].bitcast(I32), q_scales[0, :, 4 * quad:4 * quad + 4, :].bitcast(I32))
+            load_scales(nc.sync, qs, q_scales[0], quad)
         nc.sync.dma_start(vs_pool[0:1, :], vs[0:1, :])
         nc.sync.dma_start(pos_pool[:], pos)
-        v_view = vT.rearrange("(p h) t -> p h t", h=2)
         for c in range(2):
-            nc.sync.dma_start(v_raw[c][:], v_view[:, :, c * (T // 2):(c + 1) * (T // 2)])
+            nc.sync.dma_start(v_raw[c][:], vT[c * P:(c + 1) * P, :])
 
-        rows_ps = ps.tile([P, DV], F32, name="rows_ps", tag="y_ps1")
+        rows_ps = ps.tile([P, PACK * P], F32, name="rows_ps", tag="p_ps1")
         nc.tensor.transpose(rows_ps[:, 0:P], rows[:], ident[:])
         cols = sb.tile([P, 2 * BLOCKS], F32, name="cols")
         neg_sink = sb.tile([P, BLOCKS], F32, name="neg_sink")
@@ -81,7 +80,7 @@ def tile_attend_soft_alibi_sink_srtq256n512t1024_kernel(tc, q_words, q_scales, k
         ks = sb.tile([P, N], U8, name="ks", align_bytes=64)
         pos_g = sb.tile([P, N], F32, name="pos_g")
         vs_g = sb.tile([P, N], F32, name="vs_g")
-        scores = [ps.tile([P, N], F32, name=f"scores{b}") for b in range(BLOCKS)]
+        scores = [ps.tile([P, N], F32, name=f"scores{b}", tag=f"scores{b}") for b in range(BLOCKS)]
 
         def score_pass(o):
             for b in range(BLOCKS):
@@ -97,78 +96,84 @@ def tile_attend_soft_alibi_sink_srtq256n512t1024_kernel(tc, q_words, q_scales, k
         score_pass(1)
         nc.vector.tensor_copy(vs_g[:], vs_pool[:].indirect(offsets[:]))
         nc.vector.tensor_copy(pos_g[:], pos_pool[:].indirect(offsets[:]))
-        vs_ps = ps.tile([P, PACK, P], F32, name="vs_ps")
+        vs_ps = ps.tile([P, PACK, P], F32, name="vs_ps", tag="vs_ps")
         for t in range(PACK):
             nc.tensor.transpose(vs_ps[:, t, :], vs_g[:, t:N:PACK], ident[:])
 
-        v_pairs = sb.tile([P, 2 * T], BF16, name="v_pairs")
-        for c in range(2):
-            nc.scalar.activation(v_pairs[:, c * T:(c + 1) * T].rearrange("p (t h) -> p t h", h=2),
-                                 v_raw[c][:].rearrange("p h t -> p t h"), ACT.Copy)
+        v_cast = sb.tile([P, T], BF16, name="v_cast", tag="v_cast")
+        v_g = [sb.tile([P, N], BF16, name=f"v_g{h}", tag=f"v_g{h}") for h in range(2)]
+        v_ps = []
 
-        ROW = N + 8
+        def turn_values(h):
+            v_ps.append(ps.tile([P, 2, P], F32, name=f"v_ps{h}", tag=("v_ps0", "p_ps0")[h]))
+            for u in range(2):
+                nc.tensor.transpose(v_ps[h][:, u, :], v_g[h][:].bitcast(F32)[:, u:N // 2:2], ident[:])
+
+        nc.scalar.activation(v_cast[:], v_raw[0][:], ACT.Copy)
+        nc.scalar.activation(v_g[0][:], v_cast[:].indirect(offsets[:]), ACT.Copy)
+        turn_values(0)
+
         neg_m = [sb.tile([P, 1], F32, name=f"neg_m{b}") for b in range(BLOCKS)]
         total = [sb.tile([P, 1], F32, name=f"total{b}") for b in range(BLOCKS)]
         inv = sb.tile([P, BLOCKS], F32, name="inv")
-        p_ps = [ps.tile([P, PACK, P], F32, name=f"p_ps{b}") for b in range(BLOCKS)]
+        p_ps = [ps.tile([P, PACK, P], F32, name=f"p_ps{b}", tag=f"p_ps{b}") for b in range(BLOCKS)]
         s = [sb.tile([P, N], F32, name=f"s{b}") for b in range(BLOCKS)]
         neg_s = [sb.tile([P, N], F32, name=f"neg_s{b}", tag=f"neg_s{b}") for b in range(BLOCKS)]
-        p = sb.tile([P, BLOCKS * ROW], F32, name="p", tag="v_raw1")
         for b in range(BLOCKS):
             nc.vector.scalar_tensor_tensor(out=s[b][:], in0=pos_g[:], scalar=cols[:, b:b + 1], in1=scores[b][:],
                                            op0=ALU.mult, op1=ALU.add)
         for b in range(BLOCKS):
             nc.vector.tensor_scalar(neg_s[b][:], s[b][:], -1.0, neg_sink[:, b:b + 1], ALU.mult, ALU.min, accum_out=neg_m[b][:])
         for b in range(BLOCKS):
-            nc.scalar.activation(p[:, b * ROW:b * ROW + N].rearrange("p (t s) -> p s t", t=PACK),
+            p = sb.tile([P, PACK, P], F32, name=f"p{b}", tag=("v_cast", "neg_s0")[b])
+            nc.scalar.activation(p[:].rearrange("p t s -> p s t"),
                                  neg_s[b][:].rearrange("p (s t) -> p s t", t=PACK), ACT.Exp,
                                  bias=neg_m[b][:], scale=-1.0, accum_out=total[b][:])
             for t in range(PACK):
-                nc.tensor.transpose(p_ps[b][:, t, :], p[:, b * ROW + t * P:b * ROW + (t + 1) * P], ident[:])
-        vs_col = sb.tile([P, PACK], F32, name="vs_col", tag="neg_s0")
+                nc.tensor.transpose(p_ps[b][:, t, :], p[:, t, :], ident[:])
+        vs_col = sb.tile([P, PACK], F32, name="vs_col", tag="v_g0")
         nc.scalar.copy(vs_col[:], vs_ps[:, :, 0])
 
-        v_g = sb.tile([P, N], U32, name="v_g")
-        nc.vector.tensor_copy(v_g[:], v_pairs[:].bitcast(U32).indirect(offsets[:]))
-        v_ps = ps.tile([P, PACK, P], F32, name="v_ps")
-        for t in range(PACK):
-            nc.tensor.transpose(v_ps[:, t, :], v_g[:].bitcast(F32)[:, t:N:PACK], ident[:])
-
-        for b in range(BLOCKS):
-            sink_term = p[:, b * ROW + N:b * ROW + N + 1]
-            nc.scalar.activation(sink_term, cols[:, BLOCKS + b:BLOCKS + b + 1], ACT.Exp, bias=neg_m[b][:])
-            nc.scalar.activation(full[:, b:b + 1], total[b][:], ACT.Identity, bias=sink_term)
-
-        v_codes = sb.tile([P, DV], U32, name="v_codes", align_bytes=64)
-        v_scale = sb.tile([P, DV], U8, name="v_scale", align_bytes=64)
-        v_x = [sb.tile([P, P, PACK], BF16, name=f"v_x{h}", align_bytes=64) for h in range(2)]
-        for h in range(2):
-            nc.scalar.copy(v_x[h][:], v_ps[:].bitcast(BF16)[:, :, h * P:(h + 1) * P].rearrange("p t e -> p e t"))
+        nc.vector.tensor_copy(v_g[1][:], v_raw[1][:].indirect(offsets[:]))
 
         w_x = [sb.tile([P, P, PACK], BF16, name=f"w_x{b}", align_bytes=64) for b in range(BLOCKS)]
         w_codes = [sb.tile([P, P], U32, name=f"w_codes{b}", align_bytes=64) for b in range(BLOCKS)]
         w_scale = [sb.tile([P, P], U8, name=f"w_scale{b}", align_bytes=64) for b in range(BLOCKS)]
+        v_x = [sb.tile([P, P, PACK], BF16, name=f"v_x{h}", align_bytes=64) for h in range(2)]
+        v_codes = [sb.tile([P, P], U32, name=f"v_codes{h}", align_bytes=64) for h in range(2)]
+        v_scale = [sb.tile([P, P], U8, name=f"v_scale{h}", align_bytes=64) for h in range(2)]
 
         for b in range(BLOCKS):
             nc.vector.tensor_tensor(w_x[b][:], p_ps[b][:].rearrange("p t q -> p q t"),
                                     vs_col[:].unsqueeze(1).broadcast_to([P, P, PACK]), ALU.mult)
-        for b in range(BLOCKS):
-            nc.vector.quantize_mx(out=w_codes[b][:].bitcast(FP8X4), scales=w_scale[b][:],
-                                  in_=w_x[b][:].rearrange("p q t -> p (q t)"))
-        nc.vector.reciprocal(inv[:], full[:])
-        for h in range(2):
-            rng = slice(h * P, (h + 1) * P)
-            nc.vector.quantize_mx(out=v_codes[:, rng].bitcast(FP8X4), scales=v_scale[:, rng],
-                                  in_=v_x[h][:].rearrange("p e t -> p (e t)"))
+        turn_values(1)
 
+        sink_term = sb.tile([P, BLOCKS], F32, name="sink_term", tag="neg_s1")
+        nc.scalar.copy(v_x[0][:].bitcast(F32), v_ps[0][:].rearrange("p u e -> p e u"))
         for b in range(BLOCKS):
-            y_ps = ps.tile([P, DV], F32, name=f"y_ps{b}", tag=f"y_ps{b}")
-            nc.tensor.matmul_mx(out=y_ps[:], lhsT=w_codes[b][:].bitcast(FP8X4), lhsT_scale=w_scale[b][:],
-                                rhs=v_codes[:].bitcast(FP8X4), rhs_scale=v_scale[:], start=True, stop=True)
-            y = sb.tile([P, DV], F32, name=f"y{b}")
-            if b == 0:
-                nc.scalar.activation(y[:], y_ps[:], ACT.Copy, scale=inv[:, b:b + 1])
-                nc.scalar.dma_start(out[0, b * P:(b + 1) * P, :], y[:])
-            else:
-                nc.vector.tensor_scalar(y[:], y_ps[:], inv[:, b:b + 1], None, ALU.mult)
-                nc.sync.dma_start(out[0, b * P:(b + 1) * P, :], y[:])
+            nc.scalar.activation(sink_term[:, b:b + 1], cols[:, BLOCKS + b:BLOCKS + b + 1], ACT.Exp, bias=neg_m[b][:])
+        for b in range(BLOCKS):
+            nc.scalar.activation(full[:, b:b + 1], total[b][:], ACT.Identity, bias=sink_term[:, b:b + 1])
+        nc.scalar.copy(v_x[1][:].bitcast(F32), v_ps[1][:].rearrange("p u e -> p e u"))
+
+        def quantise(codes, scale, values):
+            nc.vector.quantize_mx(out=codes[:].bitcast(FP8X4), scales=scale[:], in_=values[:].rearrange("p c t -> p (c t)"))
+
+        quantise(w_codes[0], w_scale[0], w_x[0])
+        quantise(v_codes[0], v_scale[0], v_x[0])
+        quantise(w_codes[1], w_scale[1], w_x[1])
+        nc.vector.reciprocal(inv[:], full[:])
+        quantise(v_codes[1], v_scale[1], v_x[1])
+
+        y = [sb.tile([P, DV], F32, name=f"y{b}") for b in range(BLOCKS)]
+        for h in range(2):
+            for b in range(BLOCKS):
+                y_ps = ps.tile([P, P], F32, name=f"y_ps{b}{h}", tag=(("scores0", "scores1"), ("vs_ps", "v_ps0"))[h][b])
+                nc.tensor.matmul_mx(out=y_ps[:], lhsT=w_codes[b][:].bitcast(FP8X4), lhsT_scale=w_scale[b][:],
+                                    rhs=v_codes[h][:].bitcast(FP8X4), rhs_scale=v_scale[h][:], start=True, stop=True)
+                if b == 0:
+                    nc.scalar.activation(y[b][:, h * P:(h + 1) * P], y_ps[:], ACT.Copy, scale=inv[:, b:b + 1])
+                else:
+                    nc.vector.tensor_scalar(y[b][:, h * P:(h + 1) * P], y_ps[:], inv[:, b:b + 1], None, ALU.mult)
+        nc.scalar.dma_start(out[0, 0:P, :], y[0][:])
+        nc.sync.dma_start(out[0, P:2 * P, :], y[1][:])

@@ -72,9 +72,10 @@ def tile_attend_soft_alibi_sink_srtq256n512t1024_kernel(tc, q_words, q_scales, k
         rows_ps = ps.tile([P, PACK * P], F32, name="rows_ps", tag="p_ps1")
         nc.tensor.transpose(rows_ps[:, 0:P], rows[:], ident[:])
         cols = sb.tile([P, 2 * BLOCKS], F32, name="cols")
-        neg_sink = sb.tile([P, BLOCKS], F32, name="neg_sink")
+        s = [sb.tile([P, N + 1], F32, name=f"s{b}", tag=f"s{b}") for b in range(BLOCKS)]
         nc.scalar.copy(cols[:], rows_ps[:, 0:2 * BLOCKS])
-        nc.scalar.activation(neg_sink[:], rows_ps[:, BLOCKS:2 * BLOCKS], ACT.Copy, scale=-1.0)
+        for b in range(BLOCKS):
+            nc.scalar.copy(s[b][:, N:N + 1], rows_ps[:, BLOCKS + b:BLOCKS + b + 1])
 
         kw = [sb.tile([P, N], U32, name=f"kw{o}", align_bytes=64) for o in range(PASSES)]
         ks = sb.tile([P, N], U8, name="ks", align_bytes=64)
@@ -112,27 +113,25 @@ def tile_attend_soft_alibi_sink_srtq256n512t1024_kernel(tc, q_words, q_scales, k
         nc.scalar.activation(v_cast[:], v_raw[0][:], ACT.Copy)
         nc.scalar.activation(v_g[0][:], v_cast[:].indirect(offsets[:]), ACT.Copy)
         turn_values(0)
+        vs_col = sb.tile([P, PACK], F32, name="vs_col", tag="v_g0")
+        nc.scalar.copy(vs_col[:], vs_ps[:, :, 0])
 
         neg_m = [sb.tile([P, 1], F32, name=f"neg_m{b}") for b in range(BLOCKS)]
         total = [sb.tile([P, 1], F32, name=f"total{b}") for b in range(BLOCKS)]
         inv = sb.tile([P, BLOCKS], F32, name="inv")
         p_ps = [ps.tile([P, PACK, P], F32, name=f"p_ps{b}", tag=f"p_ps{b}") for b in range(BLOCKS)]
-        s = [sb.tile([P, N], F32, name=f"s{b}") for b in range(BLOCKS)]
-        neg_s = [sb.tile([P, N], F32, name=f"neg_s{b}", tag=f"neg_s{b}") for b in range(BLOCKS)]
         for b in range(BLOCKS):
-            nc.vector.scalar_tensor_tensor(out=s[b][:], in0=pos_g[:], scalar=cols[:, b:b + 1], in1=scores[b][:],
+            nc.vector.scalar_tensor_tensor(out=s[b][:, 0:N], in0=pos_g[:], scalar=cols[:, b:b + 1], in1=scores[b][:],
                                            op0=ALU.mult, op1=ALU.add)
         for b in range(BLOCKS):
-            nc.vector.tensor_scalar(neg_s[b][:], s[b][:], -1.0, neg_sink[:, b:b + 1], ALU.mult, ALU.min, accum_out=neg_m[b][:])
+            nc.vector.tensor_reduce(neg_m[b][:], s[b][:], AXIS.X, ALU.max, negate=True)
         for b in range(BLOCKS):
-            p = sb.tile([P, PACK, P], F32, name=f"p{b}", tag=("v_cast", "neg_s0")[b])
+            p = sb.tile([P, PACK, P], F32, name=f"p{b}", tag=("v_cast", "s0")[b])
             nc.scalar.activation(p[:].rearrange("p t s -> p s t"),
-                                 neg_s[b][:].rearrange("p (s t) -> p s t", t=PACK), ACT.Exp,
-                                 bias=neg_m[b][:], scale=-1.0, accum_out=total[b][:])
+                                 s[b][:, 0:N].rearrange("p (s t) -> p s t", t=PACK), ACT.Exp,
+                                 bias=neg_m[b][:], accum_out=total[b][:])
             for t in range(PACK):
                 nc.tensor.transpose(p_ps[b][:, t, :], p[:, t, :], ident[:])
-        vs_col = sb.tile([P, PACK], F32, name="vs_col", tag="v_g0")
-        nc.scalar.copy(vs_col[:], vs_ps[:, :, 0])
 
         nc.vector.tensor_copy(v_g[1][:], v_raw[1][:].indirect(offsets[:]))
 
@@ -148,7 +147,7 @@ def tile_attend_soft_alibi_sink_srtq256n512t1024_kernel(tc, q_words, q_scales, k
                                     vs_col[:].unsqueeze(1).broadcast_to([P, P, PACK]), ALU.mult)
         turn_values(1)
 
-        sink_term = sb.tile([P, BLOCKS], F32, name="sink_term", tag="neg_s1")
+        sink_term = sb.tile([P, BLOCKS], F32, name="sink_term", tag="s1")
         nc.scalar.copy(v_x[0][:].bitcast(F32), v_ps[0][:].rearrange("p u e -> p e u"))
         for b in range(BLOCKS):
             nc.scalar.activation(sink_term[:, b:b + 1], cols[:, BLOCKS + b:BLOCKS + b + 1], ACT.Exp, bias=neg_m[b][:])
@@ -159,21 +158,21 @@ def tile_attend_soft_alibi_sink_srtq256n512t1024_kernel(tc, q_words, q_scales, k
         def quantise(codes, scale, values):
             nc.vector.quantize_mx(out=codes[:].bitcast(FP8X4), scales=scale[:], in_=values[:].rearrange("p c t -> p (c t)"))
 
-        quantise(w_codes[0], w_scale[0], w_x[0])
         quantise(v_codes[0], v_scale[0], v_x[0])
+        quantise(w_codes[0], w_scale[0], w_x[0])
         quantise(w_codes[1], w_scale[1], w_x[1])
         nc.vector.reciprocal(inv[:], full[:])
         quantise(v_codes[1], v_scale[1], v_x[1])
 
-        y = [sb.tile([P, DV], F32, name=f"y{b}") for b in range(BLOCKS)]
         for h in range(2):
             for b in range(BLOCKS):
                 y_ps = ps.tile([P, P], F32, name=f"y_ps{b}{h}", tag=(("scores0", "scores1"), ("vs_ps", "v_ps0"))[h][b])
                 nc.tensor.matmul_mx(out=y_ps[:], lhsT=w_codes[b][:].bitcast(FP8X4), lhsT_scale=w_scale[b][:],
                                     rhs=v_codes[h][:].bitcast(FP8X4), rhs_scale=v_scale[h][:], start=True, stop=True)
+                y = sb.tile([P, P], F32, name=f"y{b}{h}")
                 if b == 0:
-                    nc.scalar.activation(y[b][:, h * P:(h + 1) * P], y_ps[:], ACT.Copy, scale=inv[:, b:b + 1])
+                    nc.scalar.activation(y[:], y_ps[:], ACT.Copy, scale=inv[:, b:b + 1])
                 else:
-                    nc.vector.tensor_scalar(y[b][:, h * P:(h + 1) * P], y_ps[:], inv[:, b:b + 1], None, ALU.mult)
-        nc.scalar.dma_start(out[0, 0:P, :], y[0][:])
-        nc.sync.dma_start(out[0, P:2 * P, :], y[1][:])
+                    nc.vector.tensor_scalar(y[:], y_ps[:], inv[:, b:b + 1], None, ALU.mult)
+                queue = nc.scalar if (b, h) == (0, 1) else nc.sync
+                queue.dma_start(out[0, b * P:(b + 1) * P, h * P:(h + 1) * P], y[:])

@@ -16,9 +16,12 @@ AXIS = mybir.AxisListType
 
 P = 128
 PACK = 4
+QUADS = 4
 N, T, D, DV, NQ = 512, 1024, 1024, 256, 256
 PASSES = D // (P * PACK)
 BLOCKS = NQ // P
+HALVES = DV // P
+PIECES = 2
 FLOPS = 2 * NQ * N * (D + DV)
 
 
@@ -45,29 +48,31 @@ def tile_attend_soft_alibi_sink_srtq256n512t1024_kernel(tc, q_words, q_scales, k
         kw_pool = [sb.tile([P, T], U32, name=f"kw_pool{o}") for o in range(PASSES)]
         pos_pool = sb.tile([P, T], F32, name="pos_pool")
         qw = sb.tile([P, PASSES, NQ], U32, name="qw", align_bytes=64)
-        v_raw = [sb.tile([P, T], F32, name=f"v_raw{c}") for c in range(2)]
-        full = sb.tile([P, BLOCKS], F32, name="full")
+        piece = T // PIECES
+        v0_raw = [sb.tile([P, piece], F32, name=f"v0_raw{c}") for c in range(PIECES)]
+        v1_pool = sb.tile([P, T], F32, name="v1_pool")
 
         def load_scales(queue, tile, source, quad):
-            queue.dma_start(tile[32 * quad:32 * quad + 8, :].bitcast(I32), source[:, 4 * quad:4 * quad + 4, :].bitcast(I32))
+            queue.dma_start(tile[32 * quad:32 * quad + 4 * PASSES, :].bitcast(I32),
+                            source[:, 4 * quad:4 * quad + 4, :].bitcast(I32))
 
         def load_keys(o):
             nc.sync.dma_start(kw_pool[o][:].bitcast(I32), k_words[o].rearrange("p t r -> p (t r)").bitcast(I32))
 
-        for quad in range(4):
+        for quad in range(QUADS):
             load_scales((nc.scalar, nc.sync)[quad % 2], ks_pool, k_scales, quad)
-        nc.scalar.activation(full[:, 0:1], ident[:, 0:1], ACT.Exp)
         load_keys(0)
         nc.sync.dma_start(rows[0:BLOCKS, :], slope[0, :, 0].rearrange("(b p) -> b p", p=P))
         nc.sync.dma_start(rows[BLOCKS:2 * BLOCKS, :], sink[0, :, 0].rearrange("(b p) -> b p", p=P))
         load_keys(1)
         nc.sync.dma_start(qw[:].bitcast(I32), q_words[0].rearrange("o p q r -> p o (q r)").bitcast(I32))
-        for quad in range(4):
+        for quad in range(QUADS):
             load_scales(nc.sync, qs, q_scales[0], quad)
         nc.sync.dma_start(vs_pool[0:1, :], vs[0:1, :])
         nc.sync.dma_start(pos_pool[:], pos)
-        for c in range(2):
-            nc.sync.dma_start(v_raw[c][:], vT[c * P:(c + 1) * P, :])
+        for c in range(PIECES):
+            nc.sync.dma_start(v0_raw[c][:], vT[0:P, c * piece:(c + 1) * piece])
+        nc.sync.dma_start(v1_pool[:], vT[P:2 * P, :])
 
         rows_ps = ps.tile([P, PACK * P], F32, name="rows_ps", tag="p_ps1")
         nc.tensor.transpose(rows_ps[:, 0:P], rows[:], ident[:])
@@ -82,43 +87,40 @@ def tile_attend_soft_alibi_sink_srtq256n512t1024_kernel(tc, q_words, q_scales, k
         pos_g = sb.tile([P, N], F32, name="pos_g")
         vs_g = sb.tile([P, N], F32, name="vs_g")
         scores = [ps.tile([P, N], F32, name=f"scores{b}", tag=f"scores{b}") for b in range(BLOCKS)]
-
-        def score_pass(o):
-            for b in range(BLOCKS):
-                rng = slice(b * P, (b + 1) * P)
-                nc.tensor.matmul_mx(out=scores[b][:], lhsT=qw[:, o, rng].bitcast(FP8X4), lhsT_scale=qs[4 * o:P, rng],
-                                    rhs=kw[o][:].bitcast(FP8X4), rhs_scale=ks[4 * o:P, :],
-                                    start=(o == 0), stop=(o == PASSES - 1))
-
         nc.vector.tensor_copy(ks[:], ks_pool[:].indirect(offsets[:]))
-        nc.vector.tensor_copy(kw[0][:], kw_pool[0][:].indirect(offsets[:]))
-        nc.vector.tensor_copy(kw[1][:], kw_pool[1][:].indirect(offsets[:]))
-        score_pass(0)
-        score_pass(1)
+        for o in range(PASSES):
+            nc.vector.tensor_copy(kw[o][:], kw_pool[o][:].indirect(offsets[:]))
+        for o in range(PASSES):
+            for b in range(BLOCKS):
+                queries = slice(b * P, (b + 1) * P)
+                nc.tensor.matmul_mx(out=scores[b][:], lhsT=qw[:, o, queries].bitcast(FP8X4),
+                                    lhsT_scale=qs[4 * o:P, queries], rhs=kw[o][:].bitcast(FP8X4),
+                                    rhs_scale=ks[4 * o:P, :], start=(o == 0), stop=(o == PASSES - 1))
         nc.vector.tensor_copy(vs_g[:], vs_pool[:].indirect(offsets[:]))
         nc.vector.tensor_copy(pos_g[:], pos_pool[:].indirect(offsets[:]))
+
         vs_ps = ps.tile([P, PACK, P], F32, name="vs_ps", tag="vs_ps")
         for t in range(PACK):
             nc.tensor.transpose(vs_ps[:, t, :], vs_g[:, t:N:PACK], ident[:])
 
-        v_cast = sb.tile([P, T], BF16, name="v_cast", tag="v_cast")
-        v_g = [sb.tile([P, N], BF16, name=f"v_g{h}", tag=f"v_g{h}") for h in range(2)]
+        v0_pool = sb.tile([P, T], BF16, name="v0_pool", tag="v0_pool")
+        v_g = [sb.tile([P, N], BF16, name=f"v_g{h}", tag=f"v_g{h}") for h in range(HALVES)]
         v_ps = []
 
-        def turn_values(h):
-            v_ps.append(ps.tile([P, 2, P], F32, name=f"v_ps{h}", tag=("v_ps0", "p_ps0")[h]))
+        def turn_values(h, bank):
+            v_ps.append(ps.tile([P, 2, P], F32, name=f"v_ps{h}", tag=bank))
             for u in range(2):
                 nc.tensor.transpose(v_ps[h][:, u, :], v_g[h][:].bitcast(F32)[:, u:N // 2:2], ident[:])
 
-        nc.scalar.activation(v_cast[:], v_raw[0][:], ACT.Copy)
-        nc.scalar.activation(v_g[0][:], v_cast[:].indirect(offsets[:]), ACT.Copy)
-        turn_values(0)
+        for c in range(PIECES):
+            nc.scalar.activation(v0_pool[:, c * piece:(c + 1) * piece], v0_raw[c][:], ACT.Copy)
+        nc.scalar.activation(v_g[0][:], v0_pool[:].indirect(offsets[:]), ACT.Copy)
+        turn_values(0, "v_ps0")
         vs_col = sb.tile([P, PACK], F32, name="vs_col", tag="v_g0")
         nc.scalar.copy(vs_col[:], vs_ps[:, :, 0])
 
         neg_m = [sb.tile([P, 1], F32, name=f"neg_m{b}") for b in range(BLOCKS)]
-        total = [sb.tile([P, 1], F32, name=f"total{b}") for b in range(BLOCKS)]
-        inv = sb.tile([P, BLOCKS], F32, name="inv")
+        p_sum = [sb.tile([P, 1], F32, name=f"p_sum{b}") for b in range(BLOCKS)]
         p_ps = [ps.tile([P, PACK, P], F32, name=f"p_ps{b}", tag=f"p_ps{b}") for b in range(BLOCKS)]
         for b in range(BLOCKS):
             nc.vector.scalar_tensor_tensor(out=s[b][:, 0:N], in0=pos_g[:], scalar=cols[:, b:b + 1], in1=scores[b][:],
@@ -126,53 +128,54 @@ def tile_attend_soft_alibi_sink_srtq256n512t1024_kernel(tc, q_words, q_scales, k
         for b in range(BLOCKS):
             nc.vector.tensor_reduce(neg_m[b][:], s[b][:], AXIS.X, ALU.max, negate=True)
         for b in range(BLOCKS):
-            p = sb.tile([P, PACK, P], F32, name=f"p{b}", tag=("v_cast", "s0")[b])
-            nc.scalar.activation(p[:].rearrange("p t s -> p s t"),
-                                 s[b][:, 0:N].rearrange("p (s t) -> p s t", t=PACK), ACT.Exp,
-                                 bias=neg_m[b][:], accum_out=total[b][:])
+            p = sb.tile([P, PACK, P], F32, name=f"p{b}", tag=("v0_pool", "s0")[b])
+            nc.scalar.activation(p[:].rearrange("q t s -> q s t"), s[b][:, 0:N].rearrange("q (s t) -> q s t", t=PACK),
+                                 ACT.Exp, bias=neg_m[b][:], accum_out=p_sum[b][:])
             for t in range(PACK):
                 nc.tensor.transpose(p_ps[b][:, t, :], p[:, t, :], ident[:])
 
-        nc.vector.tensor_copy(v_g[1][:], v_raw[1][:].indirect(offsets[:]))
+        nc.vector.tensor_copy(v_g[1][:], v1_pool[:].indirect(offsets[:]))
 
         w_x = [sb.tile([P, P, PACK], BF16, name=f"w_x{b}", align_bytes=64) for b in range(BLOCKS)]
         w_codes = [sb.tile([P, P], U32, name=f"w_codes{b}", align_bytes=64) for b in range(BLOCKS)]
         w_scale = [sb.tile([P, P], U8, name=f"w_scale{b}", align_bytes=64) for b in range(BLOCKS)]
-        v_x = [sb.tile([P, P, PACK], BF16, name=f"v_x{h}", align_bytes=64) for h in range(2)]
-        v_codes = [sb.tile([P, P], U32, name=f"v_codes{h}", align_bytes=64) for h in range(2)]
-        v_scale = [sb.tile([P, P], U8, name=f"v_scale{h}", align_bytes=64) for h in range(2)]
-
+        v_x = [sb.tile([P, P, PACK], BF16, name=f"v_x{h}", align_bytes=64) for h in range(HALVES)]
+        v_codes = [sb.tile([P, P], U32, name=f"v_codes{h}", align_bytes=64) for h in range(HALVES)]
+        v_scale = [sb.tile([P, P], U8, name=f"v_scale{h}", align_bytes=64) for h in range(HALVES)]
         for b in range(BLOCKS):
-            nc.vector.tensor_tensor(w_x[b][:], p_ps[b][:].rearrange("p t q -> p q t"),
+            nc.vector.tensor_tensor(w_x[b][:], p_ps[b][:].rearrange("s t q -> s q t"),
                                     vs_col[:].unsqueeze(1).broadcast_to([P, P, PACK]), ALU.mult)
-        turn_values(1)
+        turn_values(1, "p_ps0")
 
         sink_term = sb.tile([P, BLOCKS], F32, name="sink_term", tag="s1")
-        nc.scalar.copy(v_x[0][:].bitcast(F32), v_ps[0][:].rearrange("p u e -> p e u"))
+        row_sum = sb.tile([P, BLOCKS], F32, name="row_sum")
+        inv_sum = sb.tile([P, BLOCKS], F32, name="inv_sum")
+        nc.scalar.copy(v_x[0][:].bitcast(F32), v_ps[0][:].rearrange("s u e -> s e u"))
         for b in range(BLOCKS):
             nc.scalar.activation(sink_term[:, b:b + 1], cols[:, BLOCKS + b:BLOCKS + b + 1], ACT.Exp, bias=neg_m[b][:])
         for b in range(BLOCKS):
-            nc.scalar.activation(full[:, b:b + 1], total[b][:], ACT.Identity, bias=sink_term[:, b:b + 1])
-        nc.scalar.copy(v_x[1][:].bitcast(F32), v_ps[1][:].rearrange("p u e -> p e u"))
+            nc.scalar.activation(row_sum[:, b:b + 1], p_sum[b][:], ACT.Identity, bias=sink_term[:, b:b + 1])
+        nc.scalar.copy(v_x[1][:].bitcast(F32), v_ps[1][:].rearrange("s u e -> s e u"))
 
         def quantise(codes, scale, values):
-            nc.vector.quantize_mx(out=codes[:].bitcast(FP8X4), scales=scale[:], in_=values[:].rearrange("p c t -> p (c t)"))
+            nc.vector.quantize_mx(out=codes[:].bitcast(FP8X4), scales=scale[:], in_=values[:].rearrange("s c t -> s (c t)"))
 
         quantise(v_codes[0], v_scale[0], v_x[0])
-        quantise(w_codes[0], w_scale[0], w_x[0])
-        quantise(w_codes[1], w_scale[1], w_x[1])
-        nc.vector.reciprocal(inv[:], full[:])
+        for b in range(BLOCKS):
+            quantise(w_codes[b], w_scale[b], w_x[b])
+        nc.vector.reciprocal(inv_sum[:], row_sum[:])
         quantise(v_codes[1], v_scale[1], v_x[1])
 
-        for h in range(2):
+        free_banks = (("scores0", "scores1"), ("vs_ps", "v_ps0"))
+        for h in range(HALVES):
             for b in range(BLOCKS):
-                y_ps = ps.tile([P, P], F32, name=f"y_ps{b}{h}", tag=(("scores0", "scores1"), ("vs_ps", "v_ps0"))[h][b])
+                y_ps = ps.tile([P, P], F32, name=f"y_ps{b}{h}", tag=free_banks[h][b])
                 nc.tensor.matmul_mx(out=y_ps[:], lhsT=w_codes[b][:].bitcast(FP8X4), lhsT_scale=w_scale[b][:],
                                     rhs=v_codes[h][:].bitcast(FP8X4), rhs_scale=v_scale[h][:], start=True, stop=True)
                 y = sb.tile([P, P], F32, name=f"y{b}{h}")
                 if b == 0:
-                    nc.scalar.activation(y[:], y_ps[:], ACT.Copy, scale=inv[:, b:b + 1])
+                    nc.scalar.activation(y[:], y_ps[:], ACT.Copy, scale=inv_sum[:, b:b + 1])
                 else:
-                    nc.vector.tensor_scalar(y[:], y_ps[:], inv[:, b:b + 1], None, ALU.mult)
-                queue = nc.scalar if (b, h) == (0, 1) else nc.sync
+                    nc.vector.tensor_scalar(y[:], y_ps[:], inv_sum[:, b:b + 1], None, ALU.mult)
+                queue = nc.scalar if (b, h) == (0, HALVES - 1) else nc.sync
                 queue.dma_start(out[0, b * P:(b + 1) * P, h * P:(h + 1) * P], y[:])

from contextlib import ExitStack

import concourse.mybir as mybir
from concourse.masks import make_identity

F32 = mybir.dt.float32
BF16 = mybir.dt.bfloat16
I32 = mybir.dt.int32
U32 = mybir.dt.uint32
U16 = mybir.dt.uint16
U8 = mybir.dt.uint8
FP8X4 = mybir.dt.float8_e4m3fn_x4
ALU = mybir.AluOpType
ACT = mybir.ActivationFunctionType
AXIS = mybir.AxisListType

P = 128
PACK = 4
QUADS = 4
N, T, D, DV, NQ = 512, 1024, 1024, 256, 256
PASSES = D // (P * PACK)
BLOCKS = NQ // P
HALVES = DV // P
PIECES = 2
FLOPS = 2 * NQ * N * (D + DV)


def tile_attend_soft_alibi_sink_srtq256n512t1024_kernel(tc, q_words, q_scales, k_words, k_scales, vT, vs, pos, slope, sink, offs, out):
    nc = tc.nc
    with ExitStack() as ctx:
        sb = ctx.enter_context(tc.tile_pool(name="sb", bufs=1))
        ps = ctx.enter_context(tc.psum_pool(name="ps", bufs=1))

        offsets = sb.tile([P, N // 16], U16, name="offsets")
        nc.sync.dma_start(offsets[:], offs)

        ks_pool = sb.tile([P, T], U8, name="ks_pool", align_bytes=64)
        qs = sb.tile([P, NQ], U8, name="qs", align_bytes=64)
        rows = sb.tile([P, P], F32, name="rows")
        nc.gpsimd.memset(ks_pool[:].bitcast(I32), 0)
        nc.vector.memset(rows[:], 0.0)
        nc.vector.memset(qs[:].bitcast(I32), 0)
        ident = sb.tile([P, P], F32, name="ident")
        make_identity(nc, ident[:])
        vs_pool = sb.tile([P, T], F32, name="vs_pool")
        nc.gpsimd.memset(vs_pool[:], 0.0)

        kw_pool = [sb.tile([P, T], U32, name=f"kw_pool{o}") for o in range(PASSES)]
        pos_pool = sb.tile([P, T], F32, name="pos_pool")
        qw = sb.tile([P, PASSES, NQ], U32, name="qw", align_bytes=64)
        piece = T // PIECES
        v0_raw = [sb.tile([P, piece], F32, name=f"v0_raw{c}") for c in range(PIECES)]
        v1_pool = sb.tile([P, T], F32, name="v1_pool")

        def load_scales(queue, tile, source, quad):
            queue.dma_start(tile[32 * quad:32 * quad + 4 * PASSES, :].bitcast(I32),
                            source[:, 4 * quad:4 * quad + 4, :].bitcast(I32))

        def load_keys(o):
            nc.sync.dma_start(kw_pool[o][:].bitcast(I32), k_words[o].rearrange("p t r -> p (t r)").bitcast(I32))

        for quad in range(QUADS):
            load_scales((nc.scalar, nc.sync)[quad % 2], ks_pool, k_scales, quad)
        load_keys(0)
        nc.sync.dma_start(rows[0:BLOCKS, :], slope[0, :, 0].rearrange("(b p) -> b p", p=P))
        nc.sync.dma_start(rows[BLOCKS:2 * BLOCKS, :], sink[0, :, 0].rearrange("(b p) -> b p", p=P))
        load_keys(1)
        nc.sync.dma_start(qw[:].bitcast(I32), q_words[0].rearrange("o p q r -> p o (q r)").bitcast(I32))
        for quad in range(QUADS):
            load_scales(nc.sync, qs, q_scales[0], quad)
        nc.sync.dma_start(vs_pool[0:1, :], vs[0:1, :])
        nc.sync.dma_start(pos_pool[:], pos)
        for c in range(PIECES):
            nc.sync.dma_start(v0_raw[c][:], vT[0:P, c * piece:(c + 1) * piece])
        nc.sync.dma_start(v1_pool[:], vT[P:2 * P, :])

        rows_ps = ps.tile([P, PACK * P], F32, name="rows_ps", tag="p_ps1")
        nc.tensor.transpose(rows_ps[:, 0:P], rows[:], ident[:])
        cols = sb.tile([P, 2 * BLOCKS], F32, name="cols")
        s = [sb.tile([P, N + 1], F32, name=f"s{b}", tag=f"s{b}") for b in range(BLOCKS)]
        nc.scalar.copy(cols[:], rows_ps[:, 0:2 * BLOCKS])
        for b in range(BLOCKS):
            nc.scalar.copy(s[b][:, N:N + 1], rows_ps[:, BLOCKS + b:BLOCKS + b + 1])

        kw = [sb.tile([P, N], U32, name=f"kw{o}", align_bytes=64) for o in range(PASSES)]
        ks = sb.tile([P, N], U8, name="ks", align_bytes=64)
        pos_g = sb.tile([P, N], F32, name="pos_g")
        vs_g = sb.tile([P, N], F32, name="vs_g")
        scores = [ps.tile([P, N], F32, name=f"scores{b}", tag=f"scores{b}") for b in range(BLOCKS)]
        nc.vector.tensor_copy(ks[:], ks_pool[:].indirect(offsets[:]))
        for o in range(PASSES):
            nc.vector.tensor_copy(kw[o][:], kw_pool[o][:].indirect(offsets[:]))
        for o in range(PASSES):
            for b in range(BLOCKS):
                queries = slice(b * P, (b + 1) * P)
                nc.tensor.matmul_mx(out=scores[b][:], lhsT=qw[:, o, queries].bitcast(FP8X4),
                                    lhsT_scale=qs[4 * o:P, queries], rhs=kw[o][:].bitcast(FP8X4),
                                    rhs_scale=ks[4 * o:P, :], start=(o == 0), stop=(o == PASSES - 1))
        nc.vector.tensor_copy(vs_g[:], vs_pool[:].indirect(offsets[:]))
        nc.vector.tensor_copy(pos_g[:], pos_pool[:].indirect(offsets[:]))

        vs_ps = ps.tile([P, PACK, P], F32, name="vs_ps", tag="vs_ps")
        for t in range(PACK):
            nc.tensor.transpose(vs_ps[:, t, :], vs_g[:, t:N:PACK], ident[:])

        v0_pool = sb.tile([P, T], BF16, name="v0_pool", tag="v0_pool")
        v_g = [sb.tile([P, N], BF16, name=f"v_g{h}", tag=f"v_g{h}") for h in range(HALVES)]
        v_ps = []

        def turn_values(h, bank):
            v_ps.append(ps.tile([P, 2, P], F32, name=f"v_ps{h}", tag=bank))
            for u in range(2):
                nc.tensor.transpose(v_ps[h][:, u, :], v_g[h][:].bitcast(F32)[:, u:N // 2:2], ident[:])

        for c in range(PIECES):
            nc.scalar.activation(v0_pool[:, c * piece:(c + 1) * piece], v0_raw[c][:], ACT.Copy)
        nc.scalar.activation(v_g[0][:], v0_pool[:].indirect(offsets[:]), ACT.Copy)
        turn_values(0, "v_ps0")
        vs_col = sb.tile([P, PACK], F32, name="vs_col", tag="v_g0")
        nc.scalar.copy(vs_col[:], vs_ps[:, :, 0])

        neg_m = [sb.tile([P, 1], F32, name=f"neg_m{b}") for b in range(BLOCKS)]
        p_sum = [sb.tile([P, 1], F32, name=f"p_sum{b}") for b in range(BLOCKS)]
        p_ps = [ps.tile([P, PACK, P], F32, name=f"p_ps{b}", tag=f"p_ps{b}") for b in range(BLOCKS)]
        for b in range(BLOCKS):
            nc.vector.scalar_tensor_tensor(out=s[b][:, 0:N], in0=pos_g[:], scalar=cols[:, b:b + 1], in1=scores[b][:],
                                           op0=ALU.mult, op1=ALU.add)
        for b in range(BLOCKS):
            nc.vector.tensor_reduce(neg_m[b][:], s[b][:], AXIS.X, ALU.max, negate=True)
        for b in range(BLOCKS):
            p = sb.tile([P, PACK, P], F32, name=f"p{b}", tag=("v0_pool", "s0")[b])
            nc.scalar.activation(p[:].rearrange("q t s -> q s t"), s[b][:, 0:N].rearrange("q (s t) -> q s t", t=PACK),
                                 ACT.Exp, bias=neg_m[b][:], accum_out=p_sum[b][:])
            for t in range(PACK):
                nc.tensor.transpose(p_ps[b][:, t, :], p[:, t, :], ident[:])

        nc.vector.tensor_copy(v_g[1][:], v1_pool[:].indirect(offsets[:]))

        w_x = [sb.tile([P, P, PACK], BF16, name=f"w_x{b}", align_bytes=64) for b in range(BLOCKS)]
        w_codes = [sb.tile([P, P], U32, name=f"w_codes{b}", align_bytes=64) for b in range(BLOCKS)]
        w_scale = [sb.tile([P, P], U8, name=f"w_scale{b}", align_bytes=64) for b in range(BLOCKS)]
        v_x = [sb.tile([P, P, PACK], BF16, name=f"v_x{h}", align_bytes=64) for h in range(HALVES)]
        v_codes = [sb.tile([P, P], U32, name=f"v_codes{h}", align_bytes=64) for h in range(HALVES)]
        v_scale = [sb.tile([P, P], U8, name=f"v_scale{h}", align_bytes=64) for h in range(HALVES)]
        for b in range(BLOCKS):
            nc.vector.tensor_tensor(w_x[b][:], p_ps[b][:].rearrange("s t q -> s q t"),
                                    vs_col[:].unsqueeze(1).broadcast_to([P, P, PACK]), ALU.mult)
        turn_values(1, "p_ps0")

        sink_term = sb.tile([P, BLOCKS], F32, name="sink_term", tag="s1")
        row_sum = sb.tile([P, BLOCKS], F32, name="row_sum")
        inv_sum = sb.tile([P, BLOCKS], F32, name="inv_sum")
        nc.scalar.copy(v_x[0][:].bitcast(F32), v_ps[0][:].rearrange("s u e -> s e u"))
        for b in range(BLOCKS):
            nc.scalar.activation(sink_term[:, b:b + 1], cols[:, BLOCKS + b:BLOCKS + b + 1], ACT.Exp, bias=neg_m[b][:])
        for b in range(BLOCKS):
            nc.scalar.activation(row_sum[:, b:b + 1], p_sum[b][:], ACT.Identity, bias=sink_term[:, b:b + 1])
        nc.scalar.copy(v_x[1][:].bitcast(F32), v_ps[1][:].rearrange("s u e -> s e u"))

        def quantise(codes, scale, values):
            nc.vector.quantize_mx(out=codes[:].bitcast(FP8X4), scales=scale[:], in_=values[:].rearrange("s c t -> s (c t)"))

        quantise(v_codes[0], v_scale[0], v_x[0])
        for b in range(BLOCKS):
            quantise(w_codes[b], w_scale[b], w_x[b])
        nc.vector.reciprocal(inv_sum[:], row_sum[:])
        quantise(v_codes[1], v_scale[1], v_x[1])

        free_banks = (("scores0", "scores1"), ("vs_ps", "v_ps0"))
        for h in range(HALVES):
            for b in range(BLOCKS):
                y_ps = ps.tile([P, P], F32, name=f"y_ps{b}{h}", tag=free_banks[h][b])
                nc.tensor.matmul_mx(out=y_ps[:], lhsT=w_codes[b][:].bitcast(FP8X4), lhsT_scale=w_scale[b][:],
                                    rhs=v_codes[h][:].bitcast(FP8X4), rhs_scale=v_scale[h][:], start=True, stop=True)
                y = sb.tile([P, P], F32, name=f"y{b}{h}")
                if b == 0:
                    nc.scalar.activation(y[:], y_ps[:], ACT.Copy, scale=inv_sum[:, b:b + 1])
                else:
                    nc.vector.tensor_scalar(y[:], y_ps[:], inv_sum[:, b:b + 1], None, ALU.mult)
                queue = nc.scalar if (b, h) == (0, HALVES - 1) else nc.sync
                queue.dma_start(out[0, b * P:(b + 1) * P, h * P:(h + 1) * P], y[:])
